import numpy as np
import ml_dtypes


def mxq(x, axis, fmt="e4m3"):
    dtype, down = {"e4m3": (ml_dtypes.float8_e4m3fn, 7), "e5m2": (ml_dtypes.float8_e5m2, 14)}[fmt]
    v = np.moveaxis(np.asarray(x, np.float32).astype(ml_dtypes.bfloat16).astype(np.float64), axis, -1)
    blocks = v.reshape(v.shape[:-1] + (-1, 32))
    amax = np.abs(blocks).max(-1, keepdims=True)
    byte = np.maximum(np.where(amax > 0, np.frexp(amax)[1] - 1 + 127, 0) - down, 1)
    scale = np.exp2(byte - 127.0)
    codes = (blocks / scale).astype(np.float32).astype(dtype).astype(np.float64)
    return np.moveaxis((codes * scale).reshape(v.shape), -1, axis)


WIDE = False


def mx_kscale(k):
    if not WIDE:
        return np.ones(k)
    levels = np.array([10, -10, 5, -5, 0])
    if k % 512:
        return np.exp2(np.random.permutation(np.resize(levels, k // 32))).repeat(32)
    a = np.empty((k // 512, 16))
    for p in range(k // 512):
        a[p, :8] = np.random.permutation(np.resize(levels, 8))
        for g in range(8):
            far = levels[np.abs(levels - a[p, g]) >= 10]
            a[p, g + 8] = far[np.random.randint(len(far))]
    return np.exp2(a.ravel()).repeat(32)


def f64(x):
    return np.asarray(x).astype(np.float64)


def striped8(idx):
    return np.asarray(idx).reshape(8, -1, 16).transpose(0, 2, 1).reshape(128, -1).astype(np.uint16)


def unstriped8(offs):
    return offs.reshape(8, 16, -1).transpose(0, 2, 1).reshape(8, -1).astype(np.int64)


def pick8(x, idx, run):
    r = np.arange(len(x))
    return x[r[:, None], idx[r % (8 * run) // run]]


E2M1 = np.array([0.0, 0.5, 1.0, 1.5, 2.0, 3.0, 4.0, 6.0, -0.0, -0.5, -1.0, -1.5, -2.0, -3.0, -4.0, -6.0])


def pack_weight(w, fmt):
    k, n = w.shape
    w = f64(np.asarray(w, np.float32).astype(ml_dtypes.bfloat16)).reshape(k // 32, 32, n)
    amax = np.abs(w).max(1)
    if fmt == "e4m3":
        byte = np.frexp(amax)[1] - 1 + 127 - 7
    else:
        mant, ex = np.frexp(amax / 6.0)
        byte = np.where(mant > 0.5, ex, ex - 1) + 127
    byte = np.clip(np.where(amax > 0, byte, 1), 1, 254)
    scaled = (w * np.exp2(127.0 - byte)[:, None, :]).reshape(k, n).astype(np.float32)
    by_word = np.ascontiguousarray(scaled.reshape(k // 512, 128, 4, n).transpose(0, 1, 3, 2))
    if fmt == "e4m3":
        words = by_word.astype(ml_dtypes.float8_e4m3fn).view(np.uint8)
    else:
        c = by_word.astype(ml_dtypes.float4_e2m1fn).view(np.uint8) & 0xF
        words = (c[..., 0::2] | (c[..., 1::2] << 4)).reshape(k // 512, 128, 2 * n)
    return np.ascontiguousarray(words), np.ascontiguousarray(byte.astype(np.uint8).reshape(k // 512, 16, n))


def unpack_weight(words, scales, fmt):
    g, _, n = scales.shape
    words = np.ascontiguousarray(words).reshape(g, 128, n, -1)
    if fmt == "e4m3":
        vals = words.view(ml_dtypes.float8_e4m3fn).astype(np.float64)
    else:
        nib = np.empty((g, 128, n, 4), np.uint8)
        nib[..., 0::2] = words & 0xF
        nib[..., 1::2] = words >> 4
        vals = E2M1[nib]
    vals = vals * np.repeat(np.exp2(scales.astype(np.float64) - 127.0), 8, axis=1)[..., None]
    return vals.transpose(0, 1, 3, 2).reshape(g * 512, n)


D, K, T, U, I, Q = 512, 512, 1024, 1024, 512, 128


def setup_inputs():
    n = np.random.standard_normal
    idx = np.stack([np.random.permutation(T)[:I] for _ in range(8)])
    idx2 = np.stack([np.random.permutation(U)[:I] for _ in range(8)])
    idx3 = np.stack([np.random.permutation(T)[:I] for _ in range(8)])
    idx4 = np.stack([np.random.permutation(T)[:I] for _ in range(8)])
    idx5 = np.stack([np.random.permutation(U)[:I] for _ in range(8)])
    fd = mx_kscale(D)
    fk = mx_kscale(K)
    wqp = pack_weight(n((D, K)) * 1.0 / np.sqrt(D) * fd[:, None] * fk, "e4m3")
    keysp = pack_weight(n((K, T)) * 1.0 / np.sqrt(K) / fk[:, None], "e4m3")
    notesp = pack_weight(n((D, U)) * 1.0 / np.sqrt(D) * fd[:, None], "e2m1")
    return {
        "states": (n((D, Q)) * 0.95 / fd[:, None]).astype(np.float32),
        "wq_words": wqp[0],
        "wq_scales": wqp[1],
        "keys_words": keysp[0],
        "keys_scales": keysp[1],
        "notes_words": notesp[0],
        "notes_scales": notesp[1],
        "offs": striped8(idx),
        "offs2": striped8(idx2),
        "offs3": striped8(idx3),
        "offs4": striped8(idx4),
        "offs5": striped8(idx5),
    }


def reference(states, wq_words, wq_scales, keys_words, keys_scales, notes_words, notes_scales, offs, offs2, offs3, offs4, offs5):
    idx = unstriped8(offs)
    idx2 = unstriped8(offs2)
    idx3 = unstriped8(offs3)
    idx4 = unstriped8(offs4)
    idx5 = unstriped8(offs5)
    wqu = unpack_weight(wq_words, wq_scales, "e4m3")
    keysu = unpack_weight(keys_words, keys_scales, "e4m3")
    notesu = unpack_weight(notes_words, notes_scales, "e2m1")
    statesq = mxq(f64(states), 0, "e4m3")
    qv = wqu.T @ statesq
    qvq = mxq(qv, 0, "e4m3")
    a = qvq.T @ keysu
    b = statesq.T @ notesu
    f1 = np.zeros((Q, U))
    f1[np.arange(Q)[:, None], idx2[np.arange(Q) % 128 // 16]] = pick8(a, idx, 16)
    f2 = np.zeros((Q, T))
    f2[np.arange(Q)[:, None], idx3[np.arange(Q) % 128 // 16]] = pick8(b, idx2, 16)
    bb = b - f1
    aa = a + f2
    v = pick8(aa, idx4, 16) + pick8(bb, idx5, 16)
    y = np.maximum(v, pick8(aa, idx, 16))
    return y

@@ -1,0 +1,204 @@
+from contextlib import ExitStack
+
+import concourse.mybir as mybir
+
+D, K, T, U, SLOTS, Q = 512, 512, 1024, 1024, 512, 128
+FLOPS = 2 * Q * (D * K + K * T + D * U)
+
+F32 = mybir.dt.float32
+BF16 = mybir.dt.bfloat16
+I32 = mybir.dt.int32
+U32 = mybir.dt.uint32
+U16 = mybir.dt.uint16
+U8 = mybir.dt.uint8
+FP8X4 = mybir.dt.float8_e4m3fn_x4
+FP4X4 = mybir.dt.float4_e2m1fn_x4
+ADD = mybir.AluOpType.add
+SUB = mybir.AluOpType.subtract
+MAX = mybir.AluOpType.max
+COPY = mybir.ActivationFunctionType.Copy
+
+P = 128
+PACK = 4
+HALF = SLOTS // 2
+CAST_SPLIT = 96
+
+
+def entries(offsets, first, count):
+    return offsets[:, first // 16 : (first + count) // 16]
+
+
+def load_scale_rows(nc, plane, scales):
+    for quad in range(4):
+        nc.sync.dma_start(
+            out=plane[32 * quad : 32 * quad + 4, :].bitcast(I32),
+            in_=scales[0, 4 * quad : 4 * quad + 4, :].bitcast(I32),
+        )
+
+
+def tile_attend_postboxes_madeside_kernel(
+    tc, states, wq_words, wq_scales, keys_words, keys_scales, notes_words, notes_scales,
+    offs, offs2, offs3, offs4, offs5, out,
+):
+    nc = tc.nc
+    with ExitStack() as ctx:
+        keep = ctx.enter_context(tc.tile_pool(name="keep", bufs=1))
+        psum = ctx.enter_context(tc.psum_pool(name="psum", bufs=1))
+
+        notes_plane = keep.tile([P, U], U8, align_bytes=64)
+        wq_plane = keep.tile([P, K], U8, align_bytes=64)
+        keys_plane = keep.tile([P, T], U8, align_bytes=64)
+        f1 = keep.tile([P, U], F32)
+        f2 = keep.tile([P, T], F32)
+        nc.vector.memset(wq_plane[:].bitcast(I32), 0)
+        nc.vector.memset(f2[:], 0.0)
+        nc.gpsimd.memset(f1[:], 0.0)
+
+        states_raw = keep.tile([P, PACK, Q], F32)
+        nc.sync.dma_start(out=states_raw[:], in_=states.rearrange("(p j) q -> p j q", j=PACK))
+        load_scale_rows(nc, notes_plane, notes_scales)
+        wq_rows = keep.tile([4, 4, K // 4], I32)
+        nc.sync.dma_start(
+            out=wq_rows[:], in_=wq_scales[0].bitcast(I32).rearrange("(c r) w -> r c w", r=4)
+        )
+        notes_codes = keep.tile([P, 2 * U], U8, align_bytes=64)
+        nc.sync.dma_start(out=notes_codes[:].bitcast(I32), in_=notes_words[0].bitcast(I32))
+        wq_codes = keep.tile([P, K], U32)
+        nc.sync.dma_start(
+            out=wq_codes[:].bitcast(I32),
+            in_=wq_words[0].rearrange("p n t -> p (n t)").bitcast(I32),
+        )
+        list2 = keep.tile([P, SLOTS // 16], U16)
+        nc.sync.dma_start(list2[:], offs2)
+        list3 = keep.tile([P, SLOTS // 16], U16)
+        nc.sync.dma_start(list3[:], offs3)
+        load_scale_rows(nc, keys_plane, keys_scales)
+        keys_codes = keep.tile([P, T], U32, align_bytes=64)
+        nc.sync.dma_start(
+            out=keys_codes[:].bitcast(I32),
+            in_=keys_words[0].rearrange("p n t -> p (n t)").bitcast(I32),
+        )
+        list1 = keep.tile([P, SLOTS // 16], U16)
+        nc.sync.dma_start(list1[:], offs)
+        list4 = keep.tile([P, SLOTS // 16], U16)
+        nc.sync.dma_start(list4[:], offs4)
+        list5 = keep.tile([P, SLOTS // 16], U16)
+        nc.sync.dma_start(list5[:], offs5)
+
+        states_bf = keep.tile([P, Q, PACK], BF16, align_bytes=64)
+        states_t = states_raw[:].rearrange("p j q -> p q j")
+        nc.vector.tensor_copy(out=states_bf[:, :CAST_SPLIT, :], in_=states_t[:, :CAST_SPLIT, :])
+        nc.scalar.activation(states_bf[:, CAST_SPLIT:, :], states_t[:, CAST_SPLIT:, :], COPY)
+        states_codes = keep.tile([P, Q], U32, align_bytes=64)
+        states_plane = keep.tile([P, Q], U8, align_bytes=64)
+        nc.vector.quantize_mx(
+            out=states_codes[:].bitcast(FP8X4),
+            scales=states_plane[:],
+            in_=states_bf[:].rearrange("p q j -> p (q j)"),
+        )
+
+        b_sb = keep.tile([P, U], F32)
+        b_parts = [(0, 512), (512, 256), (768, 256)]
+        b_banks = []
+        for n, (first, width) in enumerate(b_parts):
+            bank = psum.tile([P, width], F32, name="b_bank%d" % n)
+            nc.tensor.matmul_mx(
+                out=bank[:],
+                lhsT=states_codes[:].bitcast(FP8X4),
+                lhsT_scale=states_plane[:],
+                rhs=notes_codes[:, 2 * first : 2 * (first + width)].bitcast(FP4X4),
+                rhs_scale=notes_plane[:, first : first + width],
+                start=True,
+                stop=True,
+            )
+            b_banks.append(bank)
+
+        for quad in range(4):
+            nc.vector.tensor_copy(
+                out=wq_plane[32 * quad : 32 * quad + 4, :].bitcast(I32), in_=wq_rows[:, quad, :]
+            )
+        wq_plane_dealt = keep.tile([P, K], U8, align_bytes=64)
+        nc.gpsimd.tensor_copy(
+            out=wq_plane_dealt[:].rearrange("p (t m) -> p t m", t=PACK),
+            in_=wq_plane[:].rearrange("p (m t) -> p t m", t=PACK),
+        )
+        wq_dealt = keep.tile([P, K], U32, align_bytes=64, tag="shared")
+        nc.scalar.copy(
+            out=wq_dealt[:].rearrange("p (t m) -> p m t", t=PACK),
+            in_=wq_codes[:].rearrange("p (m t) -> p m t", t=PACK),
+        )
+
+        nc.vector.tensor_copy(out=b_sb[:, 0:512], in_=b_banks[0][:])
+        nc.vector.tensor_copy(out=b_sb[:, 512:768], in_=b_banks[1][:])
+        nc.scalar.copy(out=b_sb[:, 768:1024], in_=b_banks[2][:])
+
+        qv_bank = psum.tile([P, PACK, Q], F32)
+        for t in range(PACK):
+            nc.tensor.matmul_mx(
+                out=qv_bank[:, t, :],
+                lhsT=wq_dealt[:, t * P : (t + 1) * P].bitcast(FP8X4),
+                lhsT_scale=wq_plane_dealt[:, t * P : (t + 1) * P],
+                rhs=states_codes[:].bitcast(FP8X4),
+                rhs_scale=states_plane[:],
+                start=True,
+                stop=True,
+            )
+
+        b_pick0 = keep.tile([P, HALF], F32)
+        nc.vector.tensor_copy(b_pick0[:], b_sb[:].indirect(entries(list2, 0, HALF)))
+        qv_bf = keep.tile([P, Q, PACK], BF16, align_bytes=64)
+        nc.scalar.copy(out=qv_bf[:], in_=qv_bank[:].rearrange("p t q -> p q t"))
+        nc.vector.tensor_copy(f2[:].indirect(entries(list3, 0, 128)), b_pick0[:, 0:128])
+        b_pick1 = keep.tile([P, HALF], F32, align_bytes=64, tag="shared")
+        nc.scalar.activation(b_pick1[:], b_sb[:].indirect(entries(list2, HALF, HALF)), COPY)
+        qv_codes = keep.tile([P, Q], U32, align_bytes=64)
+        qv_plane = keep.tile([P, Q], U8, align_bytes=64)
+        nc.vector.quantize_mx(
+            out=qv_codes[:].bitcast(FP8X4),
+            scales=qv_plane[:],
+            in_=qv_bf[:].rearrange("p q j -> p (q j)"),
+        )
+        nc.vector.tensor_copy(f2[:].indirect(entries(list3, HALF, HALF)), b_pick1[:])
+        nc.vector.tensor_copy(f2[:].indirect(entries(list3, 128, 128)), b_pick0[:, 128:256])
+
+        a_sb = keep.tile([P, T], F32)
+        for n in range(2):
+            cols = slice(512 * n, 512 * (n + 1))
+            bank = psum.tile([P, 512], F32, name="a_bank%d" % n)
+            nc.tensor.matmul_mx(
+                out=bank[:],
+                lhsT=qv_codes[:].bitcast(FP8X4),
+                lhsT_scale=qv_plane[:],
+                rhs=keys_codes[:, cols].bitcast(FP8X4),
+                rhs_scale=keys_plane[:, cols],
+                start=True,
+                stop=True,
+            )
+            nc.scalar.copy(out=a_sb[:, cols], in_=bank[:])
+
+        for h in range(2):
+            a_pick = keep.tile([P, HALF], F32, name="a_pick%d" % h)
+            nc.scalar.activation(a_pick[:], a_sb[:].indirect(entries(list1, h * HALF, HALF)), COPY)
+            nc.vector.tensor_copy(f1[:].indirect(entries(list2, h * HALF, HALF)), a_pick[:])
+
+        aa = keep.tile([P, T], F32)
+        nc.gpsimd.tensor_tensor(aa[:], a_sb[:], f2[:], ADD)
+        aa_by4 = keep.tile([P, SLOTS], F32)
+        nc.scalar.activation(aa_by4[:], aa[:].indirect(list4[:]), COPY)
+        aa_by1 = keep.tile([P, SLOTS], F32)
+        nc.scalar.activation(aa_by1[:], aa[:].indirect(list1[:]), COPY)
+
+        bb = keep.tile([P, U], F32)
+        for (first, width), bank in zip(b_parts, b_banks):
+            cols = slice(first, first + width)
+            nc.vector.tensor_tensor(bb[:, cols], bank[:], f1[:, cols], SUB)
+
+        for h in range(2):
+            cols = slice(h * HALF, (h + 1) * HALF)
+            v = keep.tile([P, HALF], F32, name="v%d" % h)
+            nc.vector.tensor_tensor(
+                v[:], bb[:].indirect(entries(list5, h * HALF, HALF)), aa_by4[:, cols], ADD
+            )
+            y = keep.tile([P, HALF], F32, name="y%d" % h)
+            nc.vector.tensor_tensor(y[:], v[:], aa_by1[:, cols], MAX)
+            nc.sync.dma_start(out=out[:, cols], in_=y[:])

@@ -15,6 +15,7 @@ FP8X4 = mybir.dt.float8_e4m3fn_x4
 FP4X4 = mybir.dt.float4_e2m1fn_x4
 ADD = mybir.AluOpType.add
 SUB = mybir.AluOpType.subtract
+MULT = mybir.AluOpType.mult
 MAX = mybir.AluOpType.max
 COPY = mybir.ActivationFunctionType.Copy
 
@@ -22,6 +23,8 @@ P = 128
 PACK = 4
 HALF = SLOTS // 2
 CAST_SPLIT = 96
+FIRST = 128
+REST = SLOTS - FIRST
 
 
 def entries(offsets, first, count):
@@ -52,7 +55,9 @@ def tile_attend_postboxes_madeside_kernel(
         f2 = keep.tile([P, T], F32)
         nc.vector.memset(wq_plane[:].bitcast(I32), 0)
         nc.vector.memset(f2[:], 0.0)
-        nc.gpsimd.memset(f1[:], 0.0)
+        ones = keep.tile([P, FIRST], F32)
+        nc.vector.memset(ones[:], 1.0)
+        nc.vector.memset(f1[:], 0.0)
 
         states_raw = keep.tile([P, PACK, Q], F32)
         nc.sync.dma_start(out=states_raw[:], in_=states.rearrange("(p j) q -> p j q", j=PACK))
@@ -72,12 +77,12 @@ def tile_attend_postboxes_madeside_kernel(
         nc.sync.dma_start(list2[:], offs2)
         list3 = keep.tile([P, SLOTS // 16], U16)
         nc.sync.dma_start(list3[:], offs3)
-        load_scale_rows(nc, keys_plane, keys_scales)
         keys_codes = keep.tile([P, T], U32, align_bytes=64)
         nc.sync.dma_start(
             out=keys_codes[:].bitcast(I32),
             in_=keys_words[0].rearrange("p n t -> p (n t)").bitcast(I32),
         )
+        load_scale_rows(nc, keys_plane, keys_scales)
         list1 = keep.tile([P, SLOTS // 16], U16)
         nc.sync.dma_start(list1[:], offs)
         list4 = keep.tile([P, SLOTS // 16], U16)
@@ -118,7 +123,7 @@ def tile_attend_postboxes_madeside_kernel(
                 out=wq_plane[32 * quad : 32 * quad + 4, :].bitcast(I32), in_=wq_rows[:, quad, :]
             )
         wq_plane_dealt = keep.tile([P, K], U8, align_bytes=64)
-        nc.gpsimd.tensor_copy(
+        nc.vector.tensor_copy(
             out=wq_plane_dealt[:].rearrange("p (t m) -> p t m", t=PACK),
             in_=wq_plane[:].rearrange("p (m t) -> p t m", t=PACK),
         )
@@ -144,13 +149,15 @@ def tile_attend_postboxes_madeside_kernel(
                 stop=True,
             )
 
-        b_pick0 = keep.tile([P, HALF], F32)
-        nc.vector.tensor_copy(b_pick0[:], b_sb[:].indirect(entries(list2, 0, HALF)))
+        b_pick0 = keep.tile([P, FIRST], F32)
+        nc.vector.tensor_tensor(
+            b_pick0[:], b_sb[:].indirect(entries(list2, 0, FIRST)), ones[:], MULT
+        )
         qv_bf = keep.tile([P, Q, PACK], BF16, align_bytes=64)
         nc.scalar.copy(out=qv_bf[:], in_=qv_bank[:].rearrange("p t q -> p q t"))
-        nc.vector.tensor_copy(f2[:].indirect(entries(list3, 0, 128)), b_pick0[:, 0:128])
-        b_pick1 = keep.tile([P, HALF], F32, align_bytes=64, tag="shared")
-        nc.scalar.activation(b_pick1[:], b_sb[:].indirect(entries(list2, HALF, HALF)), COPY)
+        nc.vector.tensor_copy(f2[:].indirect(entries(list3, 0, FIRST)), b_pick0[:])
+        b_pick1 = keep.tile([P, REST], F32, align_bytes=64, tag="shared")
+        nc.scalar.activation(b_pick1[:], b_sb[:].indirect(entries(list2, FIRST, REST)), COPY)
         qv_codes = keep.tile([P, Q], U32, align_bytes=64)
         qv_plane = keep.tile([P, Q], U8, align_bytes=64)
         nc.vector.quantize_mx(
@@ -158,13 +165,12 @@ def tile_attend_postboxes_madeside_kernel(
             scales=qv_plane[:],
             in_=qv_bf[:].rearrange("p q j -> p (q j)"),
         )
-        nc.vector.tensor_copy(f2[:].indirect(entries(list3, HALF, HALF)), b_pick1[:])
-        nc.vector.tensor_copy(f2[:].indirect(entries(list3, 128, 128)), b_pick0[:, 128:256])
+        nc.vector.tensor_copy(f2[:].indirect(entries(list3, FIRST, REST)), b_pick1[:])
 
         a_sb = keep.tile([P, T], F32)
-        for n in range(2):
-            cols = slice(512 * n, 512 * (n + 1))
-            bank = psum.tile([P, 512], F32, name="a_bank%d" % n)
+        for n in range(4):
+            cols = slice(256 * n, 256 * (n + 1))
+            bank = psum.tile([P, 256], F32, name="a_bank%d" % n)
             nc.tensor.matmul_mx(
                 out=bank[:],
                 lhsT=qv_codes[:].bitcast(FP8X4),
@@ -183,22 +189,27 @@ def tile_attend_postboxes_madeside_kernel(
 
         aa = keep.tile([P, T], F32)
         nc.gpsimd.tensor_tensor(aa[:], a_sb[:], f2[:], ADD)
+        halves = [slice(0, HALF), slice(HALF, SLOTS)]
         aa_by4 = keep.tile([P, SLOTS], F32)
-        nc.scalar.activation(aa_by4[:], aa[:].indirect(list4[:]), COPY)
         aa_by1 = keep.tile([P, SLOTS], F32)
-        nc.scalar.activation(aa_by1[:], aa[:].indirect(list1[:]), COPY)
+        for picked, offsets in ((aa_by4, list4), (aa_by1, list1)):
+            for cols in halves:
+                nc.scalar.activation(
+                    picked[:, cols], aa[:].indirect(entries(offsets, cols.start, HALF)), COPY
+                )
 
         bb = keep.tile([P, U], F32)
-        for (first, width), bank in zip(b_parts, b_banks):
+        for (first, width), bank in zip(b_parts[:2], b_banks[:2]):
             cols = slice(first, first + width)
             nc.vector.tensor_tensor(bb[:, cols], bank[:], f1[:, cols], SUB)
+        nc.gpsimd.tensor_tensor(bb[:, 768:], b_sb[:, 768:], f1[:, 768:], SUB)
 
-        for h in range(2):
-            cols = slice(h * HALF, (h + 1) * HALF)
-            v = keep.tile([P, HALF], F32, name="v%d" % h)
+        v = keep.tile([P, SLOTS], F32)
+        for cols in halves:
             nc.vector.tensor_tensor(
-                v[:], bb[:].indirect(entries(list5, h * HALF, HALF)), aa_by4[:, cols], ADD
+                v[:, cols], bb[:].indirect(entries(list5, cols.start, HALF)), aa_by4[:, cols], ADD
             )
-            y = keep.tile([P, HALF], F32, name="y%d" % h)
-            nc.vector.tensor_tensor(y[:], v[:], aa_by1[:, cols], MAX)
-            nc.sync.dma_start(out=out[:, cols], in_=y[:])
+        y = keep.tile([P, SLOTS], F32)
+        for cols, queue in zip(halves, (nc.sync, nc.scalar)):
+            nc.vector.tensor_tensor(y[:, cols], v[:, cols], aa_by1[:, cols], MAX)
+            queue.dma_start(out=out[:, cols], in_=y[:, cols])

from contextlib import ExitStack

import concourse.mybir as mybir

D, K, T, U, SLOTS, Q = 512, 512, 1024, 1024, 512, 128
FLOPS = 2 * Q * (D * K + K * T + D * U)

F32 = mybir.dt.float32
BF16 = mybir.dt.bfloat16
I32 = mybir.dt.int32
U32 = mybir.dt.uint32
U16 = mybir.dt.uint16
U8 = mybir.dt.uint8
FP8X4 = mybir.dt.float8_e4m3fn_x4
FP4X4 = mybir.dt.float4_e2m1fn_x4
ADD = mybir.AluOpType.add
SUB = mybir.AluOpType.subtract
MULT = mybir.AluOpType.mult
MAX = mybir.AluOpType.max
COPY = mybir.ActivationFunctionType.Copy

P = 128
PACK = 4
HALF = SLOTS // 2
CAST_SPLIT = 96
FIRST = 128
REST = SLOTS - FIRST


def entries(offsets, first, count):
    return offsets[:, first // 16 : (first + count) // 16]


def load_scale_rows(nc, plane, scales):
    for quad in range(4):
        nc.sync.dma_start(
            out=plane[32 * quad : 32 * quad + 4, :].bitcast(I32),
            in_=scales[0, 4 * quad : 4 * quad + 4, :].bitcast(I32),
        )


def tile_attend_postboxes_madeside_kernel(
    tc, states, wq_words, wq_scales, keys_words, keys_scales, notes_words, notes_scales,
    offs, offs2, offs3, offs4, offs5, out,
):
    nc = tc.nc
    with ExitStack() as ctx:
        keep = ctx.enter_context(tc.tile_pool(name="keep", bufs=1))
        psum = ctx.enter_context(tc.psum_pool(name="psum", bufs=1))

        notes_plane = keep.tile([P, U], U8, align_bytes=64)
        wq_plane = keep.tile([P, K], U8, align_bytes=64)
        keys_plane = keep.tile([P, T], U8, align_bytes=64)
        f1 = keep.tile([P, U], F32)
        f2 = keep.tile([P, T], F32)
        nc.vector.memset(wq_plane[:].bitcast(I32), 0)
        nc.vector.memset(f2[:], 0.0)
        ones = keep.tile([P, FIRST], F32)
        nc.vector.memset(ones[:], 1.0)
        nc.vector.memset(f1[:], 0.0)

        states_raw = keep.tile([P, PACK, Q], F32)
        nc.sync.dma_start(out=states_raw[:], in_=states.rearrange("(p j) q -> p j q", j=PACK))
        load_scale_rows(nc, notes_plane, notes_scales)
        wq_rows = keep.tile([4, 4, K // 4], I32)
        nc.sync.dma_start(
            out=wq_rows[:], in_=wq_scales[0].bitcast(I32).rearrange("(c r) w -> r c w", r=4)
        )
        notes_codes = keep.tile([P, 2 * U], U8, align_bytes=64)
        nc.sync.dma_start(out=notes_codes[:].bitcast(I32), in_=notes_words[0].bitcast(I32))
        wq_codes = keep.tile([P, K], U32)
        nc.sync.dma_start(
            out=wq_codes[:].bitcast(I32),
            in_=wq_words[0].rearrange("p n t -> p (n t)").bitcast(I32),
        )
        list2 = keep.tile([P, SLOTS // 16], U16)
        nc.sync.dma_start(list2[:], offs2)
        list3 = keep.tile([P, SLOTS // 16], U16)
        nc.sync.dma_start(list3[:], offs3)
        keys_codes = keep.tile([P, T], U32, align_bytes=64)
        nc.sync.dma_start(
            out=keys_codes[:].bitcast(I32),
            in_=keys_words[0].rearrange("p n t -> p (n t)").bitcast(I32),
        )
        load_scale_rows(nc, keys_plane, keys_scales)
        list1 = keep.tile([P, SLOTS // 16], U16)
        nc.sync.dma_start(list1[:], offs)
        list4 = keep.tile([P, SLOTS // 16], U16)
        nc.sync.dma_start(list4[:], offs4)
        list5 = keep.tile([P, SLOTS // 16], U16)
        nc.sync.dma_start(list5[:], offs5)

        states_bf = keep.tile([P, Q, PACK], BF16, align_bytes=64)
        states_t = states_raw[:].rearrange("p j q -> p q j")
        nc.vector.tensor_copy(out=states_bf[:, :CAST_SPLIT, :], in_=states_t[:, :CAST_SPLIT, :])
        nc.scalar.activation(states_bf[:, CAST_SPLIT:, :], states_t[:, CAST_SPLIT:, :], COPY)
        states_codes = keep.tile([P, Q], U32, align_bytes=64)
        states_plane = keep.tile([P, Q], U8, align_bytes=64)
        nc.vector.quantize_mx(
            out=states_codes[:].bitcast(FP8X4),
            scales=states_plane[:],
            in_=states_bf[:].rearrange("p q j -> p (q j)"),
        )

        b_sb = keep.tile([P, U], F32)
        b_parts = [(0, 512), (512, 256), (768, 256)]
        b_banks = []
        for n, (first, width) in enumerate(b_parts):
            bank = psum.tile([P, width], F32, name="b_bank%d" % n)
            nc.tensor.matmul_mx(
                out=bank[:],
                lhsT=states_codes[:].bitcast(FP8X4),
                lhsT_scale=states_plane[:],
                rhs=notes_codes[:, 2 * first : 2 * (first + width)].bitcast(FP4X4),
                rhs_scale=notes_plane[:, first : first + width],
                start=True,
                stop=True,
            )
            b_banks.append(bank)

        for quad in range(4):
            nc.vector.tensor_copy(
                out=wq_plane[32 * quad : 32 * quad + 4, :].bitcast(I32), in_=wq_rows[:, quad, :]
            )
        wq_plane_dealt = keep.tile([P, K], U8, align_bytes=64)
        nc.vector.tensor_copy(
            out=wq_plane_dealt[:].rearrange("p (t m) -> p t m", t=PACK),
            in_=wq_plane[:].rearrange("p (m t) -> p t m", t=PACK),
        )
        wq_dealt = keep.tile([P, K], U32, align_bytes=64, tag="shared")
        nc.scalar.copy(
            out=wq_dealt[:].rearrange("p (t m) -> p m t", t=PACK),
            in_=wq_codes[:].rearrange("p (m t) -> p m t", t=PACK),
        )

        nc.vector.tensor_copy(out=b_sb[:, 0:512], in_=b_banks[0][:])
        nc.vector.tensor_copy(out=b_sb[:, 512:768], in_=b_banks[1][:])
        nc.scalar.copy(out=b_sb[:, 768:1024], in_=b_banks[2][:])

        qv_bank = psum.tile([P, PACK, Q], F32)
        for t in range(PACK):
            nc.tensor.matmul_mx(
                out=qv_bank[:, t, :],
                lhsT=wq_dealt[:, t * P : (t + 1) * P].bitcast(FP8X4),
                lhsT_scale=wq_plane_dealt[:, t * P : (t + 1) * P],
                rhs=states_codes[:].bitcast(FP8X4),
                rhs_scale=states_plane[:],
                start=True,
                stop=True,
            )

        b_pick0 = keep.tile([P, FIRST], F32)
        nc.vector.tensor_tensor(
            b_pick0[:], b_sb[:].indirect(entries(list2, 0, FIRST)), ones[:], MULT
        )
        qv_bf = keep.tile([P, Q, PACK], BF16, align_bytes=64)
        nc.scalar.copy(out=qv_bf[:], in_=qv_bank[:].rearrange("p t q -> p q t"))
        nc.vector.tensor_copy(f2[:].indirect(entries(list3, 0, FIRST)), b_pick0[:])
        b_pick1 = keep.tile([P, REST], F32, align_bytes=64, tag="shared")
        nc.scalar.activation(b_pick1[:], b_sb[:].indirect(entries(list2, FIRST, REST)), COPY)
        qv_codes = keep.tile([P, Q], U32, align_bytes=64)
        qv_plane = keep.tile([P, Q], U8, align_bytes=64)
        nc.vector.quantize_mx(
            out=qv_codes[:].bitcast(FP8X4),
            scales=qv_plane[:],
            in_=qv_bf[:].rearrange("p q j -> p (q j)"),
        )
        nc.vector.tensor_copy(f2[:].indirect(entries(list3, FIRST, REST)), b_pick1[:])

        a_sb = keep.tile([P, T], F32)
        for n in range(4):
            cols = slice(256 * n, 256 * (n + 1))
            bank = psum.tile([P, 256], F32, name="a_bank%d" % n)
            nc.tensor.matmul_mx(
                out=bank[:],
                lhsT=qv_codes[:].bitcast(FP8X4),
                lhsT_scale=qv_plane[:],
                rhs=keys_codes[:, cols].bitcast(FP8X4),
                rhs_scale=keys_plane[:, cols],
                start=True,
                stop=True,
            )
            nc.scalar.copy(out=a_sb[:, cols], in_=bank[:])

        for h in range(2):
            a_pick = keep.tile([P, HALF], F32, name="a_pick%d" % h)
            nc.scalar.activation(a_pick[:], a_sb[:].indirect(entries(list1, h * HALF, HALF)), COPY)
            nc.vector.tensor_copy(f1[:].indirect(entries(list2, h * HALF, HALF)), a_pick[:])

        aa = keep.tile([P, T], F32)
        nc.gpsimd.tensor_tensor(aa[:], a_sb[:], f2[:], ADD)
        halves = [slice(0, HALF), slice(HALF, SLOTS)]
        aa_by4 = keep.tile([P, SLOTS], F32)
        aa_by1 = keep.tile([P, SLOTS], F32)
        for picked, offsets in ((aa_by4, list4), (aa_by1, list1)):
            for cols in halves:
                nc.scalar.activation(
                    picked[:, cols], aa[:].indirect(entries(offsets, cols.start, HALF)), COPY
                )

        bb = keep.tile([P, U], F32)
        for (first, width), bank in zip(b_parts[:2], b_banks[:2]):
            cols = slice(first, first + width)
            nc.vector.tensor_tensor(bb[:, cols], bank[:], f1[:, cols], SUB)
        nc.gpsimd.tensor_tensor(bb[:, 768:], b_sb[:, 768:], f1[:, 768:], SUB)

        v = keep.tile([P, SLOTS], F32)
        for cols in halves:
            nc.vector.tensor_tensor(
                v[:, cols], bb[:].indirect(entries(list5, cols.start, HALF)), aa_by4[:, cols], ADD
            )
        y = keep.tile([P, SLOTS], F32)
        for cols, queue in zip(halves, (nc.sync, nc.scalar)):
            nc.vector.tensor_tensor(y[:, cols], v[:, cols], aa_by1[:, cols], MAX)
            queue.dma_start(out=out[:, cols], in_=y[:, cols])
